import numpy as np
import ml_dtypes


def mxq(x, axis, fmt="e4m3"):
    dtype, down = {"e4m3": (ml_dtypes.float8_e4m3fn, 7), "e5m2": (ml_dtypes.float8_e5m2, 14)}[fmt]
    v = np.moveaxis(np.asarray(x, np.float32).astype(ml_dtypes.bfloat16).astype(np.float64), axis, -1)
    blocks = v.reshape(v.shape[:-1] + (-1, 32))
    amax = np.abs(blocks).max(-1, keepdims=True)
    byte = np.maximum(np.where(amax > 0, np.frexp(amax)[1] - 1 + 127, 0) - down, 1)
    scale = np.exp2(byte - 127.0)
    codes = (blocks / scale).astype(np.float32).astype(dtype).astype(np.float64)
    return np.moveaxis((codes * scale).reshape(v.shape), -1, axis)


WIDE = False


def mx_kscale(k):
    if not WIDE:
        return np.ones(k)
    levels = np.array([10, -10, 5, -5, 0])
    if k % 512:
        return np.exp2(np.random.permutation(np.resize(levels, k // 32))).repeat(32)
    a = np.empty((k // 512, 16))
    for p in range(k // 512):
        a[p, :8] = np.random.permutation(np.resize(levels, 8))
        for g in range(8):
            far = levels[np.abs(levels - a[p, g]) >= 10]
            a[p, g + 8] = far[np.random.randint(len(far))]
    return np.exp2(a.ravel()).repeat(32)


def f64(x):
    return np.asarray(x).astype(np.float64)


def striped(idx):
    return np.tile(np.asarray(idx).reshape(-1, 16).T, (8, 1)).astype(np.uint16)


def unstriped(offs):
    return offs[:16].T.reshape(-1).astype(np.int64)


E2M1 = np.array([0.0, 0.5, 1.0, 1.5, 2.0, 3.0, 4.0, 6.0, -0.0, -0.5, -1.0, -1.5, -2.0, -3.0, -4.0, -6.0])


def pack_weight(w, fmt):
    k, n = w.shape
    w = f64(np.asarray(w, np.float32).astype(ml_dtypes.bfloat16)).reshape(k // 32, 32, n)
    amax = np.abs(w).max(1)
    if fmt == "e4m3":
        byte = np.frexp(amax)[1] - 1 + 127 - 7
    else:
        mant, ex = np.frexp(amax / 6.0)
        byte = np.where(mant > 0.5, ex, ex - 1) + 127
    byte = np.clip(np.where(amax > 0, byte, 1), 1, 254)
    scaled = (w * np.exp2(127.0 - byte)[:, None, :]).reshape(k, n).astype(np.float32)
    by_word = np.ascontiguousarray(scaled.reshape(k // 512, 128, 4, n).transpose(0, 1, 3, 2))
    if fmt == "e4m3":
        words = by_word.astype(ml_dtypes.float8_e4m3fn).view(np.uint8)
    else:
        c = by_word.astype(ml_dtypes.float4_e2m1fn).view(np.uint8) & 0xF
        words = (c[..., 0::2] | (c[..., 1::2] << 4)).reshape(k // 512, 128, 2 * n)
    return np.ascontiguousarray(words), np.ascontiguousarray(byte.astype(np.uint8).reshape(k // 512, 16, n))


def unpack_weight(words, scales, fmt):
    g, _, n = scales.shape
    words = np.ascontiguousarray(words).reshape(g, 128, n, -1)
    if fmt == "e4m3":
        vals = words.view(ml_dtypes.float8_e4m3fn).astype(np.float64)
    else:
        nib = np.empty((g, 128, n, 4), np.uint8)
        nib[..., 0::2] = words & 0xF
        nib[..., 1::2] = words >> 4
        vals = E2M1[nib]
    vals = vals * np.repeat(np.exp2(scales.astype(np.float64) - 127.0), 8, axis=1)[..., None]
    return vals.transpose(0, 1, 3, 2).reshape(g * 512, n)


D, E, T, I, Q, G = 512, 512, 2048, 512, 256, 32


def setup_inputs():
    n = np.random.standard_normal
    idx = np.random.permutation(T)[:I]
    fd = mx_kscale(D)
    fi = mx_kscale(I)
    ti = np.ones(T)
    ti[idx] = fi
    keysp = pack_weight(n((D, T)) / fd[:, None], "e4m3")
    return {
        "query": (n((D, Q)) * 0.7 / np.sqrt(D) * fd[:, None]).astype(np.float32),
        "dquery": (n((D, Q)) * 1.0 / np.sqrt(D) * fd[:, None]).astype(np.float32),
        "keys_words": keysp[0],
        "keys_scales": keysp[1],
        "reserve": (np.random.uniform(1.0, 8.0, (I, 1))).astype(np.float32),
        "os": (np.random.uniform(0.1, 0.4, (I, 1)) * fi[:, None]).astype(np.float32),
        "vals": (n((E, T)) / ti).astype(np.float32),
        "offs": striped(idx),
    }


def reference(query, dquery, keys_words, keys_scales, reserve, os, vals, offs):
    idx = unstriped(offs)
    keysu = unpack_weight(keys_words, keys_scales, "e4m3")
    keysidxg = keysu[:, idx]
    queryq = mxq(f64(query), 0, "e4m3")
    a = keysidxg.T @ queryq
    dqueryq = mxq(f64(dquery), 0, "e4m3")
    ta = keysidxg.T @ dqueryq
    p = np.exp(a)
    s = 1.0 / (p.reshape(I, G, Q // G).sum(axis=2) + f64(reserve))
    sr = np.repeat(s, Q // G, axis=1)
    tp = ta * p
    ts = tp.reshape(I, G, Q // G).sum(axis=2) * (-1.0) / np.square(p.reshape(I, G, Q // G).sum(axis=2) + f64(reserve))
    tsr = np.repeat(ts, Q // G, axis=1)
    tw = tp * sr + tsr * p
    wo1 = tw * f64(os)
    vt1 = f64(vals)[:, idx].T
    wo1q = mxq(wo1, 0, "e4m3")
    vt1q = mxq(vt1, 0, "e4m3")
    o = wo1q.T @ vt1q
    return o

@@ -1,0 +1,209 @@
+from contextlib import ExitStack
+
+import concourse.mybir as mybir
+from concourse.masks import make_identity
+
+D, E, T, I, Q, G = 512, 512, 2048, 512, 256, 32
+FLOPS = 2 * (2 * D * I * Q + I * Q * E)
+
+F32 = mybir.dt.float32
+BF16 = mybir.dt.bfloat16
+I32 = mybir.dt.int32
+U32 = mybir.dt.uint32
+U16 = mybir.dt.uint16
+U8 = mybir.dt.uint8
+FP8X4 = mybir.dt.float8_e4m3fn_x4
+ALU = mybir.AluOpType
+ACT = mybir.ActivationFunctionType
+
+P = 128
+PACK = 4
+TEAM = Q // G
+HALF = TEAM // 2
+
+
+def tile_attend_ttteamshares_kernel(tc, query, dquery, keys_words, keys_scales, reserve, slot_factor, vals, offs, out):
+    nc = tc.nc
+    with ExitStack() as ctx:
+        keep = ctx.enter_context(tc.tile_pool(name="keep", bufs=1))
+        psum = ctx.enter_context(tc.psum_pool(name="psum", bufs=1))
+
+        offsets = keep.tile([P, I // 16], U16, name="offsets")
+        nc.sync.dma_start(offsets[:], offs)
+
+        key_scale_pool = keep.tile([P, T], U8, name="key_scale_pool", align_bytes=64)
+        nc.vector.memset(key_scale_pool[:].bitcast(I32), 0)
+        for quad in range(4):
+            nc.sync.dma_start(
+                key_scale_pool[32 * quad : 32 * quad + 4, :].bitcast(I32),
+                keys_scales[0, 4 * quad : 4 * quad + 4, :].bitcast(I32),
+            )
+        q_raw = keep.tile([P, PACK, Q], F32, name="q_raw")
+        nc.sync.dma_start(q_raw[:], query.rearrange("(p t) q -> p t q", t=PACK))
+        key_pool = keep.tile([P, T], I32, name="key_pool")
+        nc.sync.dma_start(key_pool[:], keys_words[0].rearrange("p n t -> p (n t)").bitcast(I32))
+        dq_raw = keep.tile([P, PACK, Q], F32, name="dq_raw")
+        nc.sync.dma_start(dq_raw[:], dquery.rearrange("(p t) q -> p t q", t=PACK))
+        val_pools = []
+        for k in range(E // P):
+            val_pool = keep.tile([P, T], F32, name=f"val_pool{k}", tag=f"val_pool{k}", align_bytes=64)
+            nc.sync.dma_start(val_pool[:], vals[k * P : (k + 1) * P, :])
+            val_pools.append(val_pool)
+
+        reserve_t = keep.tile([P, 1, PACK], F32, name="reserve_t")
+        nc.gpsimd.dma_start(reserve_t[:], reserve.rearrange("(p t) o -> p o t", t=PACK))
+        os_t = keep.tile([P, 1, PACK], F32, name="os_t", tag="os_t", align_bytes=64)
+        nc.gpsimd.dma_start(os_t[:], slot_factor.rearrange("(p t) o -> p o t", t=PACK))
+        identity = keep.tile([P, P], F32, name="identity")
+        make_identity(nc, identity[:])
+        reserve_wide = keep.tile([P, G, PACK], F32, name="reserve_wide")
+        nc.gpsimd.tensor_copy(reserve_wide[:], reserve_t[:].to_broadcast([P, G, PACK]))
+
+        key_scales_listed = keep.tile([P, I], U8, name="key_scales_listed", align_bytes=64)
+        nc.vector.tensor_copy(key_scales_listed[:], key_scale_pool[:].indirect(offsets[:]))
+        key_scales = keep.tile([P, PACK, P], U8, name="key_scales", align_bytes=64)
+        nc.vector.tensor_copy(
+            key_scales[:].rearrange("p t (a b) -> p a t b", b=16),
+            key_scales_listed[:].rearrange("p (a b t) -> p a t b", b=16, t=PACK),
+        )
+
+        def interleave(copy, raw, name):
+            grouped = keep.tile([P, Q * PACK], BF16, name=name, align_bytes=64)
+            copy(
+                grouped[:].rearrange("p (h g l t) -> p h g t l", h=2, l=HALF, t=PACK),
+                raw[:].rearrange("p t (g h l) -> p h g t l", h=2, l=HALF),
+            )
+            return grouped
+
+        def quantise(grouped, width, name, tag=None):
+            codes = keep.tile([P, width], U32, name=name + "_codes", tag=tag or name + "_codes", align_bytes=64)
+            scales = keep.tile([P, width], U8, name=name + "_scales", align_bytes=64)
+            nc.vector.quantize_mx(out=codes[:].bitcast(FP8X4), scales=scales[:], in_=grouped)
+            return codes, scales
+
+        q_grouped = interleave(nc.scalar.copy, q_raw, "q_grouped")
+        q_codes, q_scales = quantise(q_grouped[:], Q, "q")
+
+        key_codes = keep.tile([P, PACK, P], U32, name="key_codes", align_bytes=64)
+        nc.vector.tensor_copy(
+            key_codes[:].rearrange("p t s -> p s t"), key_pool[:].bitcast(U32).indirect(offsets[:])
+        )
+
+        def scores(codes, scales, tag):
+            banks = []
+            for h in range(2):
+                bank = psum.tile([P, PACK, P], F32, name=f"{tag}{h}", tag=f"{tag}{h}")
+                for t in range(PACK):
+                    nc.tensor.matmul_mx(
+                        out=bank[:, t, :],
+                        lhsT=key_codes[:, t, :].bitcast(FP8X4),
+                        lhsT_scale=key_scales[:, t, :],
+                        rhs=codes[:, h * P : (h + 1) * P].bitcast(FP8X4),
+                        rhs_scale=scales[:, h * P : (h + 1) * P],
+                        start=True,
+                        stop=True,
+                    )
+                banks.append(bank[:].rearrange("p t (g l) -> p l g t", l=HALF))
+            return banks
+
+        a_banks = scores(q_codes, q_scales, "a")
+        dq_grouped = interleave(nc.vector.tensor_copy, dq_raw, "dq_grouped")
+        dq_codes, dq_scales = quantise(dq_grouped[:], Q, "dq")
+        ta_banks = scores(dq_codes, dq_scales, "ta")
+
+        p_all = keep.tile([P, TEAM, G, PACK], F32, name="p_all")
+        halves = [slice(h * HALF, (h + 1) * HALF) for h in range(2)]
+        for h in range(2):
+            nc.scalar.activation(p_all[:, halves[h], :, :], a_banks[h], ACT.Exp)
+
+        def team_sum(members, name):
+            turned = psum.tile([P, P], F32, name=name + "_turned", tag=name + "_turned")
+            for n, member in enumerate(members):
+                nc.tensor.matmul(
+                    turned[:], member, identity[:], is_transpose=True, start=(n == 0), stop=(n == len(members) - 1)
+                )
+            staged = keep.tile([P, P], F32, name=name + "_staged")
+            nc.scalar.copy(staged[:], turned[:])
+            total = psum.tile([P, 1, G * PACK], F32, name=name + "_total", tag="total")
+            nc.tensor.transpose(total[:, 0, :], staged[:], identity[:])
+            return total
+
+        def members_of(tile):
+            return [tile[:, j, :, :].rearrange("p g t -> p (g t)") for j in range(TEAM)]
+
+        val_grouped = [keep.tile([P, 2, P * PACK], BF16, name=f"val_grouped{n}", align_bytes=64) for n in range(2)]
+
+        def gather_values(k, listed_tag, bank_tag):
+            listed = keep.tile([P, I], BF16, name=f"val_listed{k}", tag=listed_tag, align_bytes=64)
+            nc.vector.tensor_copy(listed[:], val_pools[k][:].indirect(offsets[:]))
+            words = listed[:].bitcast(F32)
+            turned = psum.tile([P, 2, P], F32, name=f"val_turned{k}", tag=bank_tag)
+            for u in range(2):
+                nc.tensor.transpose(turned[:, u, :], words[:, u::2], identity[:])
+            nc.scalar.copy(
+                val_grouped[k // 2][:, k % 2, :].bitcast(F32).rearrange("p (e u) -> p e u", u=2),
+                turned[:].rearrange("p u e -> p e u"),
+            )
+
+        den = team_sum([reserve_wide[:].rearrange("p g t -> p (g t)")] + members_of(p_all), "den")
+        gather_values(0, "val_listed0", "den_turned")
+        tp_all = keep.tile([P, TEAM, G, PACK], F32, name="tp_all", tag="val_pool0", align_bytes=64)
+        for h in range(2):
+            nc.vector.tensor_tensor(tp_all[:, halves[h], :, :], ta_banks[h], p_all[:, halves[h], :, :], ALU.mult)
+        share = keep.tile([P, 1, G * PACK], F32, name="share", tag="share", align_bytes=64)
+        nc.vector.reciprocal(share[:], den[:])
+        factor = keep.tile([P, 1, G * PACK], F32, name="factor")
+        nc.vector.tensor_tensor(
+            factor[:].rearrange("p o (g t) -> p (o g) t", t=PACK),
+            share[:].rearrange("p o (g t) -> p (o g) t", t=PACK),
+            os_t[:].to_broadcast([P, G, PACK]),
+            ALU.mult,
+        )
+        weighted = keep.tile([P, TEAM, G * PACK], F32, name="weighted")
+        nc.gpsimd.tensor_tensor(
+            weighted[:],
+            p_all[:].rearrange("p j g t -> p j (g t)"),
+            factor[:].to_broadcast([P, TEAM, G * PACK]),
+            ALU.mult,
+        )
+        tp_sum = team_sum(members_of(tp_all), "tp")
+        gather_values(1, "os_t", "tp_turned")
+        mean = keep.tile([P, 1, G, PACK], F32, name="mean", tag="val_pool1", align_bytes=64)
+        nc.vector.tensor_tensor(mean[:].rearrange("p o g t -> p o (g t)"), tp_sum[:], share[:], ALU.mult)
+        gather_values(2, "share", "den_turned")
+        centred = keep.tile([P, TEAM, G, PACK], F32, name="centred", tag="val_pool2", align_bytes=64)
+        for h in range(2):
+            nc.vector.tensor_tensor(
+                centred[:, halves[h], :, :], ta_banks[h], mean[:].to_broadcast([P, HALF, G, PACK]), ALU.subtract
+            )
+        val_mx = [quantise(val_grouped[0][:].rearrange("p k x -> p (k x)"), 2 * P, "val0", "val_pool0")]
+        gather_values(3, "val_pool1", "spare")
+        w_grouped = keep.tile([P, 2, G // 2, TEAM, PACK], BF16, name="w_grouped", tag="val_pool3", align_bytes=64)
+        for h in range(2):
+            teams = slice(h * G // 2, (h + 1) * G // 2)
+            nc.vector.tensor_tensor(
+                w_grouped[:, h, :, :, :],
+                centred[:].rearrange("p j g t -> p g j t")[:, teams, :, :],
+                weighted[:].rearrange("p j (g t) -> p g j t", t=PACK)[:, teams, :, :],
+                ALU.mult,
+            )
+        w_mx = [quantise(w_grouped[:, 0, :, :, :].rearrange("p g j t -> p (g j t)"), P, "w0")]
+        val_mx.append(quantise(val_grouped[1][:].rearrange("p k x -> p (k x)"), 2 * P, "val1", "val_pool2"))
+        w_mx.append(quantise(w_grouped[:, 1, :, :, :].rearrange("p g j t -> p (g j t)"), P, "w1"))
+
+        for h in range(2):
+            result = keep.tile([P, 2, 2 * P], F32, name=f"result{h}")
+            for n in range(2):
+                bank = psum.tile([P, 2 * P], F32, name=f"out_bank{h}{n}", tag=["a0", "a1", "ta0", "ta1"][2 * h + n])
+                nc.tensor.matmul_mx(
+                    out=bank[:],
+                    lhsT=w_mx[h][0][:].bitcast(FP8X4),
+                    lhsT_scale=w_mx[h][1][:],
+                    rhs=val_mx[n][0][:].bitcast(FP8X4),
+                    rhs_scale=val_mx[n][1][:],
+                    start=True,
+                    stop=True,
+                )
+                copy = nc.vector.tensor_copy if n == 1 else nc.scalar.copy
+                copy(result[:, n, :], bank[:])
+            nc.sync.dma_start(out[h * P : (h + 1) * P, :], result[:].rearrange("p n e -> p (n e)"))

@@ -20,12 +20,14 @@ P = 128
 PACK = 4
 TEAM = Q // G
 HALF = TEAM // 2
+POOL_BYTES = T * 4
 
 
 def tile_attend_ttteamshares_kernel(tc, query, dquery, keys_words, keys_scales, reserve, slot_factor, vals, offs, out):
     nc = tc.nc
     with ExitStack() as ctx:
         keep = ctx.enter_context(tc.tile_pool(name="keep", bufs=1))
+        shared = ctx.enter_context(tc.tile_pool(name="shared", bufs=1))
         psum = ctx.enter_context(tc.psum_pool(name="psum", bufs=1))
 
         offsets = keep.tile([P, I // 16], U16, name="offsets")
@@ -46,7 +48,7 @@ def tile_attend_ttteamshares_kernel(tc, query, dquery, keys_words, keys_scales, 
         nc.sync.dma_start(dq_raw[:], dquery.rearrange("(p t) q -> p t q", t=PACK))
         val_pools = []
         for k in range(E // P):
-            val_pool = keep.tile([P, T], F32, name=f"val_pool{k}", tag=f"val_pool{k}", align_bytes=64)
+            val_pool = shared.tile([P, T], F32, name=f"val_pool{k}", offset=k * POOL_BYTES, align_bytes=64)
             nc.sync.dma_start(val_pool[:], vals[k * P : (k + 1) * P, :])
             val_pools.append(val_pool)
 
@@ -56,7 +58,7 @@ def tile_attend_ttteamshares_kernel(tc, query, dquery, keys_words, keys_scales, 
         nc.gpsimd.dma_start(os_t[:], slot_factor.rearrange("(p t) o -> p o t", t=PACK))
         identity = keep.tile([P, P], F32, name="identity")
         make_identity(nc, identity[:])
-        reserve_wide = keep.tile([P, G, PACK], F32, name="reserve_wide")
+        reserve_wide = keep.tile([P, G, PACK], F32, name="reserve_wide", tag="reserve_wide", align_bytes=64)
         nc.gpsimd.tensor_copy(reserve_wide[:], reserve_t[:].to_broadcast([P, G, PACK]))
 
         key_scales_listed = keep.tile([P, I], U8, name="key_scales_listed", align_bytes=64)
@@ -75,8 +77,11 @@ def tile_attend_ttteamshares_kernel(tc, query, dquery, keys_words, keys_scales, 
             )
             return grouped
 
-        def quantise(grouped, width, name, tag=None):
-            codes = keep.tile([P, width], U32, name=name + "_codes", tag=tag or name + "_codes", align_bytes=64)
+        def quantise(grouped, width, name, offset=None):
+            if offset is None:
+                codes = keep.tile([P, width], U32, name=name + "_codes", align_bytes=64)
+            else:
+                codes = shared.tile([P, width], U32, name=name + "_codes", offset=offset, align_bytes=64)
             scales = keep.tile([P, width], U8, name=name + "_scales", align_bytes=64)
             nc.vector.quantize_mx(out=codes[:].bitcast(FP8X4), scales=scales[:], in_=grouped)
             return codes, scales
@@ -116,25 +121,26 @@ def tile_attend_ttteamshares_kernel(tc, query, dquery, keys_words, keys_scales, 
         for h in range(2):
             nc.scalar.activation(p_all[:, halves[h], :, :], a_banks[h], ACT.Exp)
 
-        def team_sum(members, name):
-            turned = psum.tile([P, P], F32, name=name + "_turned", tag=name + "_turned")
+        def team_sum(members, name, tag):
+            turned = psum.tile([P, P], F32, name=name + "_turned", tag=tag)
             for n, member in enumerate(members):
                 nc.tensor.matmul(
                     turned[:], member, identity[:], is_transpose=True, start=(n == 0), stop=(n == len(members) - 1)
                 )
-            staged = keep.tile([P, P], F32, name=name + "_staged")
-            nc.scalar.copy(staged[:], turned[:])
-            total = psum.tile([P, 1, G * PACK], F32, name=name + "_total", tag="total")
-            nc.tensor.transpose(total[:, 0, :], staged[:], identity[:])
-            return total
+            return turned
+
+        def turn_back(turned, name):
+            back = psum.tile([P, G, PACK], F32, name=name, tag="back")
+            nc.tensor.transpose(back[:].rearrange("p g t -> p (g t)"), turned[:], identity[:])
+            return back
 
         def members_of(tile):
             return [tile[:, j, :, :].rearrange("p g t -> p (g t)") for j in range(TEAM)]
 
         val_grouped = [keep.tile([P, 2, P * PACK], BF16, name=f"val_grouped{n}", align_bytes=64) for n in range(2)]
 
-        def gather_values(k, listed_tag, bank_tag):
-            listed = keep.tile([P, I], BF16, name=f"val_listed{k}", tag=listed_tag, align_bytes=64)
+        def gather_values(k, bank_tag):
+            listed = keep.tile([P, I], BF16, name=f"val_listed{k}", tag=["val_listed0", "reserve_wide", "os_t", "val_listed3"][k], align_bytes=64)
             nc.vector.tensor_copy(listed[:], val_pools[k][:].indirect(offsets[:]))
             words = listed[:].bitcast(F32)
             turned = psum.tile([P, 2, P], F32, name=f"val_turned{k}", tag=bank_tag)
@@ -145,17 +151,26 @@ def tile_attend_ttteamshares_kernel(tc, query, dquery, keys_words, keys_scales, 
                 turned[:].rearrange("p u e -> p e u"),
             )
 
-        den = team_sum([reserve_wide[:].rearrange("p g t -> p (g t)")] + members_of(p_all), "den")
-        gather_values(0, "val_listed0", "den_turned")
-        tp_all = keep.tile([P, TEAM, G, PACK], F32, name="tp_all", tag="val_pool0", align_bytes=64)
+        den = team_sum(members_of(p_all) + [reserve_wide[:].rearrange("p g t -> p (g t)")], "den", "den")
+        root_turned = keep.tile([P, P], F32, name="root_turned")
+        nc.scalar.activation(root_turned[:], den[:], ACT.Abs_reciprocal_sqrt)
+        sign_turned = keep.tile([P, P], F32, name="sign_turned")
+        nc.scalar.activation(sign_turned[:], den[:], ACT.Sign)
+        size_turned = keep.tile([P, P], F32, name="size_turned")
+        nc.scalar.activation(size_turned[:], root_turned[:], ACT.Square)
+        share_turned = keep.tile([P, P], F32, name="share_turned")
+        nc.gpsimd.tensor_tensor(share_turned[:], size_turned[:], sign_turned[:], ALU.mult)
+        share = turn_back(share_turned, "share")
+        gather_values(0, "den")
+        tp_all = shared.tile([P, TEAM, G, PACK], F32, name="tp_all", offset=0, align_bytes=64)
         for h in range(2):
             nc.vector.tensor_tensor(tp_all[:, halves[h], :, :], ta_banks[h], p_all[:, halves[h], :, :], ALU.mult)
-        share = keep.tile([P, 1, G * PACK], F32, name="share", tag="share", align_bytes=64)
-        nc.vector.reciprocal(share[:], den[:])
-        factor = keep.tile([P, 1, G * PACK], F32, name="factor")
+        tp_sum = team_sum(members_of(tp_all), "tp", "a1")
+        gather_values(1, "val_a")
+        factor = shared.tile([P, 1, G * PACK], F32, name="factor", offset=POOL_BYTES, align_bytes=64)
         nc.vector.tensor_tensor(
             factor[:].rearrange("p o (g t) -> p (o g) t", t=PACK),
-            share[:].rearrange("p o (g t) -> p (o g) t", t=PACK),
+            share[:],
             os_t[:].to_broadcast([P, G, PACK]),
             ALU.mult,
         )
@@ -166,19 +181,22 @@ def tile_attend_ttteamshares_kernel(tc, query, dquery, keys_words, keys_scales, 
             factor[:].to_broadcast([P, TEAM, G * PACK]),
             ALU.mult,
         )
-        tp_sum = team_sum(members_of(tp_all), "tp")
-        gather_values(1, "os_t", "tp_turned")
-        mean = keep.tile([P, 1, G, PACK], F32, name="mean", tag="val_pool1", align_bytes=64)
-        nc.vector.tensor_tensor(mean[:].rearrange("p o g t -> p o (g t)"), tp_sum[:], share[:], ALU.mult)
-        gather_values(2, "share", "den_turned")
-        centred = keep.tile([P, TEAM, G, PACK], F32, name="centred", tag="val_pool2", align_bytes=64)
+        mean_turned = shared.tile([P, P], F32, name="mean_turned", offset=POOL_BYTES + 1024, align_bytes=64)
+        nc.vector.tensor_tensor(mean_turned[:], tp_sum[:], share_turned[:], ALU.mult)
+        mean_back = turn_back(mean_turned, "mean_back")
+        mean = keep.tile([P, 1, G, PACK], F32, name="mean")
+        nc.scalar.copy(mean[:, 0, :, :], mean_back[:])
+        gather_values(2, "val_b")
+        val_mx = [quantise(val_grouped[0][:].rearrange("p k x -> p (k x)"), 2 * P, "val0", 2 * POOL_BYTES + 4096)]
+        centred = shared.tile([P, TEAM, G, PACK], F32, name="centred", offset=2 * POOL_BYTES, align_bytes=64)
         for h in range(2):
             nc.vector.tensor_tensor(
                 centred[:, halves[h], :, :], ta_banks[h], mean[:].to_broadcast([P, HALF, G, PACK]), ALU.subtract
             )
-        val_mx = [quantise(val_grouped[0][:].rearrange("p k x -> p (k x)"), 2 * P, "val0", "val_pool0")]
-        gather_values(3, "val_pool1", "spare")
-        w_grouped = keep.tile([P, 2, G // 2, TEAM, PACK], BF16, name="w_grouped", tag="val_pool3", align_bytes=64)
+        gather_values(3, "val_a")
+        w_grouped = shared.tile(
+            [P, 2, G // 2, TEAM, PACK], BF16, name="w_grouped", offset=3 * POOL_BYTES, align_bytes=64
+        )
         for h in range(2):
             teams = slice(h * G // 2, (h + 1) * G // 2)
             nc.vector.tensor_tensor(
@@ -188,7 +206,7 @@ def tile_attend_ttteamshares_kernel(tc, query, dquery, keys_words, keys_scales, 
                 ALU.mult,
             )
         w_mx = [quantise(w_grouped[:, 0, :, :, :].rearrange("p g j t -> p (g j t)"), P, "w0")]
-        val_mx.append(quantise(val_grouped[1][:].rearrange("p k x -> p (k x)"), 2 * P, "val1", "val_pool2"))
+        val_mx.append(quantise(val_grouped[1][:].rearrange("p k x -> p (k x)"), 2 * P, "val1", 2 * POOL_BYTES))
         w_mx.append(quantise(w_grouped[:, 1, :, :, :].rearrange("p g j t -> p (g j t)"), P, "w1"))
 
         for h in range(2):

@@ -116,7 +116,7 @@ def tile_attend_ttteamshares_kernel(tc, query, dquery, keys_words, keys_scales, 
         dq_codes, dq_scales = quantise(dq_grouped[:], Q, "dq")
         ta_banks = scores(dq_codes, dq_scales, "ta")
 
-        p_all = keep.tile([P, TEAM, G, PACK], F32, name="p_all")
+        p_all = keep.tile([P, TEAM, G, PACK], F32, name="p_all", tag="p_all", align_bytes=64)
         halves = [slice(h * HALF, (h + 1) * HALF) for h in range(2)]
         for h in range(2):
             nc.scalar.activation(p_all[:, halves[h], :, :], a_banks[h], ACT.Exp)
@@ -129,25 +129,42 @@ def tile_attend_ttteamshares_kernel(tc, query, dquery, keys_words, keys_scales, 
                 )
             return turned
 
-        def turn_back(turned, name):
-            back = psum.tile([P, G, PACK], F32, name=name, tag="back")
-            nc.tensor.transpose(back[:].rearrange("p g t -> p (g t)"), turned[:], identity[:])
+        def turn_back(turned, name, tag):
+            back = psum.tile([P, 1, G, PACK], F32, name=name, tag=tag)
+            nc.tensor.transpose(back[:].rearrange("p o g t -> p (o g t)"), turned[:], identity[:])
             return back
 
         def members_of(tile):
             return [tile[:, j, :, :].rearrange("p g t -> p (g t)") for j in range(TEAM)]
 
-        val_grouped = [keep.tile([P, 2, P * PACK], BF16, name=f"val_grouped{n}", align_bytes=64) for n in range(2)]
+        val_grouped = keep.tile([P, E * PACK], BF16, name="val_grouped", align_bytes=64)
+        val_scales = keep.tile([P, E], U8, name="val_scales", align_bytes=64)
+        val_codes = [keep.tile([P, 2 * P], U32, name="val_codes0", align_bytes=64)]
 
-        def gather_values(k, bank_tag):
-            listed = keep.tile([P, I], BF16, name=f"val_listed{k}", tag=["val_listed0", "reserve_wide", "os_t", "val_listed3"][k], align_bytes=64)
-            nc.vector.tensor_copy(listed[:], val_pools[k][:].indirect(offsets[:]))
+        def quantise_values(first, count):
+            nc.vector.quantize_mx(
+                out=val_codes[first // 2][:, first % 2 * P : (first % 2 + count) * P].bitcast(FP8X4),
+                scales=val_scales[:, first * P : (first + count) * P],
+                in_=val_grouped[:, first * P * PACK : (first + count) * P * PACK],
+            )
+
+        def gather_values(k):
+            listed = keep.tile([P, I], BF16, name=f"val_listed{k}", tag=["val_listed0", "reserve_wide", "val_listed2", "p_all"][k], align_bytes=64)
+            if k == 2:
+                rounded = keep.tile([P, T], BF16, name="val_rounded", tag="val_listed0", align_bytes=64)
+                nc.scalar.activation(rounded[:], val_pools[k][:], ACT.Copy)
+                nc.scalar.activation(listed[:], rounded[:].indirect(offsets[:]), ACT.Copy)
+            else:
+                nc.vector.tensor_copy(listed[:], val_pools[k][:].indirect(offsets[:]))
+            return listed
+
+        def turn_values(k, listed, bank_tag, copy_out):
             words = listed[:].bitcast(F32)
             turned = psum.tile([P, 2, P], F32, name=f"val_turned{k}", tag=bank_tag)
             for u in range(2):
                 nc.tensor.transpose(turned[:, u, :], words[:, u::2], identity[:])
-            nc.scalar.copy(
-                val_grouped[k // 2][:, k % 2, :].bitcast(F32).rearrange("p (e u) -> p e u", u=2),
+            copy_out(
+                val_grouped[:, k * P * PACK : (k + 1) * P * PACK].bitcast(F32).rearrange("p (e u) -> p e u", u=2),
                 turned[:].rearrange("p u e -> p e u"),
             )
 
@@ -156,44 +173,40 @@ def tile_attend_ttteamshares_kernel(tc, query, dquery, keys_words, keys_scales, 
         nc.scalar.activation(root_turned[:], den[:], ACT.Abs_reciprocal_sqrt)
         sign_turned = keep.tile([P, P], F32, name="sign_turned")
         nc.scalar.activation(sign_turned[:], den[:], ACT.Sign)
-        size_turned = keep.tile([P, P], F32, name="size_turned")
+        size_turned = keep.tile([P, P], F32, name="size_turned", tag="size_turned", align_bytes=64)
         nc.scalar.activation(size_turned[:], root_turned[:], ACT.Square)
-        share_turned = keep.tile([P, P], F32, name="share_turned")
-        nc.gpsimd.tensor_tensor(share_turned[:], size_turned[:], sign_turned[:], ALU.mult)
-        share = turn_back(share_turned, "share")
-        gather_values(0, "den")
+        turn_values(0, gather_values(0), "den", nc.scalar.copy)
         tp_all = shared.tile([P, TEAM, G, PACK], F32, name="tp_all", offset=0, align_bytes=64)
         for h in range(2):
             nc.vector.tensor_tensor(tp_all[:, halves[h], :, :], ta_banks[h], p_all[:, halves[h], :, :], ALU.mult)
         tp_sum = team_sum(members_of(tp_all), "tp", "a1")
-        gather_values(1, "val_a")
-        factor = shared.tile([P, 1, G * PACK], F32, name="factor", offset=POOL_BYTES, align_bytes=64)
-        nc.vector.tensor_tensor(
-            factor[:].rearrange("p o (g t) -> p (o g) t", t=PACK),
-            share[:],
-            os_t[:].to_broadcast([P, G, PACK]),
-            ALU.mult,
-        )
-        weighted = keep.tile([P, TEAM, G * PACK], F32, name="weighted")
-        nc.gpsimd.tensor_tensor(
-            weighted[:],
-            p_all[:].rearrange("p j g t -> p j (g t)"),
-            factor[:].to_broadcast([P, TEAM, G * PACK]),
-            ALU.mult,
-        )
-        mean_turned = shared.tile([P, P], F32, name="mean_turned", offset=POOL_BYTES + 1024, align_bytes=64)
+        listed1 = gather_values(1)
+        share_turned = shared.tile([P, P], F32, name="share_turned", offset=POOL_BYTES + 2048, align_bytes=64)
+        nc.vector.tensor_tensor(share_turned[:], size_turned[:], sign_turned[:], ALU.mult)
+        mean_turned = keep.tile([P, P], F32, name="mean_turned", tag="mean_turned", align_bytes=64)
         nc.vector.tensor_tensor(mean_turned[:], tp_sum[:], share_turned[:], ALU.mult)
-        mean_back = turn_back(mean_turned, "mean_back")
-        mean = keep.tile([P, 1, G, PACK], F32, name="mean")
-        nc.scalar.copy(mean[:, 0, :, :], mean_back[:])
-        gather_values(2, "val_b")
-        val_mx = [quantise(val_grouped[0][:].rearrange("p k x -> p (k x)"), 2 * P, "val0", 2 * POOL_BYTES + 4096)]
-        centred = shared.tile([P, TEAM, G, PACK], F32, name="centred", offset=2 * POOL_BYTES, align_bytes=64)
+        mean = turn_back(mean_turned, "mean", "a0")
+        share = turn_back(share_turned, "share", "back")
+        turn_values(1, listed1, "val_a", nc.vector.tensor_copy)
+        turn_values(2, gather_values(2), "val_b", nc.scalar.copy)
+        factor = keep.tile([P, G, 1, PACK], F32, name="factor")
+        nc.vector.tensor_tensor(factor[:, :, 0, :], share[:, 0, :, :], os_t[:].to_broadcast([P, G, PACK]), ALU.mult)
+        quantise_values(0, 2)
+        pull = keep.tile([P, TEAM, G, PACK], F32, name="pull")
+        centred = keep.tile([P, TEAM, G, PACK], F32, name="centred", tag="centred", align_bytes=64)
         for h in range(2):
             nc.vector.tensor_tensor(
-                centred[:, halves[h], :, :], ta_banks[h], mean[:].to_broadcast([P, HALF, G, PACK]), ALU.subtract
+                pull[:, halves[h], :, :], mean[:].to_broadcast([P, HALF, G, PACK]), p_all[:, halves[h], :, :], ALU.mult
             )
-        gather_values(3, "val_a")
+        for h in range(2):
+            nc.vector.tensor_tensor(
+                centred[:, halves[h], :, :], tp_all[:, halves[h], :, :], pull[:, halves[h], :, :], ALU.subtract
+            )
+        turn_values(3, gather_values(3), "val_a", nc.scalar.copy)
+        val_codes.append(
+            shared.tile([P, 2 * P], U32, name="val_codes1", offset=3 * POOL_BYTES + 4096, align_bytes=64)
+        )
+        quantise_values(2, 1)
         w_grouped = shared.tile(
             [P, 2, G // 2, TEAM, PACK], BF16, name="w_grouped", offset=3 * POOL_BYTES, align_bytes=64
         )
@@ -202,26 +215,26 @@ def tile_attend_ttteamshares_kernel(tc, query, dquery, keys_words, keys_scales, 
             nc.vector.tensor_tensor(
                 w_grouped[:, h, :, :, :],
                 centred[:].rearrange("p j g t -> p g j t")[:, teams, :, :],
-                weighted[:].rearrange("p j (g t) -> p g j t", t=PACK)[:, teams, :, :],
+                factor[:, teams, :, :].to_broadcast([P, G // 2, TEAM, PACK]),
                 ALU.mult,
             )
         w_mx = [quantise(w_grouped[:, 0, :, :, :].rearrange("p g j t -> p (g j t)"), P, "w0")]
-        val_mx.append(quantise(val_grouped[1][:].rearrange("p k x -> p (k x)"), 2 * P, "val1", 2 * POOL_BYTES))
+        quantise_values(3, 1)
         w_mx.append(quantise(w_grouped[:, 1, :, :, :].rearrange("p g j t -> p (g j t)"), P, "w1"))
 
         for h in range(2):
-            result = keep.tile([P, 2, 2 * P], F32, name=f"result{h}")
             for n in range(2):
-                bank = psum.tile([P, 2 * P], F32, name=f"out_bank{h}{n}", tag=["a0", "a1", "ta0", "ta1"][2 * h + n])
+                bank = psum.tile([P, 2 * P], F32, name=f"out_bank{h}{n}", tag=["ta0", "ta1", "a0", "a1"][2 * h + n])
                 nc.tensor.matmul_mx(
                     out=bank[:],
                     lhsT=w_mx[h][0][:].bitcast(FP8X4),
                     lhsT_scale=w_mx[h][1][:],
-                    rhs=val_mx[n][0][:].bitcast(FP8X4),
-                    rhs_scale=val_mx[n][1][:],
+                    rhs=val_codes[n][:].bitcast(FP8X4),
+                    rhs_scale=val_scales[:, n * 2 * P : (n + 1) * 2 * P],
                     start=True,
                     stop=True,
                 )
                 copy = nc.vector.tensor_copy if n == 1 else nc.scalar.copy
-                copy(result[:, n, :], bank[:])
-            nc.sync.dma_start(out[h * P : (h + 1) * P, :], result[:].rearrange("p n e -> p (n e)"))
+                result = keep.tile([P, 2 * P], F32, name=f"result{h}{n}")
+                copy(result[:], bank[:])
+                nc.sync.dma_start(out[h * P : (h + 1) * P, n * 2 * P : (n + 1) * 2 * P], result[:])

@@ -35,10 +35,10 @@ def tile_attend_ttteamshares_kernel(tc, query, dquery, keys_words, keys_scales, 
 
         key_scale_pool = keep.tile([P, T], U8, name="key_scale_pool", align_bytes=64)
         nc.vector.memset(key_scale_pool[:].bitcast(I32), 0)
-        for quad in range(4):
+        for row in range(4):
             nc.sync.dma_start(
-                key_scale_pool[32 * quad : 32 * quad + 4, :].bitcast(I32),
-                keys_scales[0, 4 * quad : 4 * quad + 4, :].bitcast(I32),
+                key_scale_pool[row:P:32, :].bitcast(I32),
+                keys_scales[0, row:16:4, :].bitcast(I32),
             )
         q_raw = keep.tile([P, PACK, Q], F32, name="q_raw")
         nc.sync.dma_start(q_raw[:], query.rearrange("(p t) q -> p t q", t=PACK))
@@ -61,6 +61,12 @@ def tile_attend_ttteamshares_kernel(tc, query, dquery, keys_words, keys_scales, 
         reserve_wide = keep.tile([P, G, PACK], F32, name="reserve_wide", tag="reserve_wide", align_bytes=64)
         nc.gpsimd.tensor_copy(reserve_wide[:], reserve_t[:].to_broadcast([P, G, PACK]))
 
+        os_wide = keep.tile([P, G, PACK], F32, name="os_wide")
+        nc.gpsimd.tensor_copy(os_wide[:], os_t[:].to_broadcast([P, G, PACK]))
+        os_bank = psum.tile([P, P], F32, name="os_bank", tag="back")
+        nc.tensor.transpose(os_bank[:], os_wide[:].rearrange("p g t -> p (g t)"), identity[:])
+        os_turned = keep.tile([P, P], F32, name="os_turned")
+        nc.scalar.copy(os_turned[:], os_bank[:])
         key_scales_listed = keep.tile([P, I], U8, name="key_scales_listed", align_bytes=64)
         nc.vector.tensor_copy(key_scales_listed[:], key_scale_pool[:].indirect(offsets[:]))
         key_scales = keep.tile([P, PACK, P], U8, name="key_scales", align_bytes=64)
@@ -175,6 +181,8 @@ def tile_attend_ttteamshares_kernel(tc, query, dquery, keys_words, keys_scales, 
         nc.scalar.activation(sign_turned[:], den[:], ACT.Sign)
         size_turned = keep.tile([P, P], F32, name="size_turned", tag="size_turned", align_bytes=64)
         nc.scalar.activation(size_turned[:], root_turned[:], ACT.Square)
+        signed_os = keep.tile([P, P], F32, name="signed_os")
+        nc.gpsimd.tensor_tensor(signed_os[:], sign_turned[:], os_turned[:], ALU.mult)
         turn_values(0, gather_values(0), "den", nc.scalar.copy)
         tp_all = shared.tile([P, TEAM, G, PACK], F32, name="tp_all", offset=0, align_bytes=64)
         for h in range(2):
@@ -183,43 +191,40 @@ def tile_attend_ttteamshares_kernel(tc, query, dquery, keys_words, keys_scales, 
         listed1 = gather_values(1)
         share_turned = shared.tile([P, P], F32, name="share_turned", offset=POOL_BYTES + 2048, align_bytes=64)
         nc.vector.tensor_tensor(share_turned[:], size_turned[:], sign_turned[:], ALU.mult)
+        factor_turned = shared.tile([P, P], F32, name="factor_turned", offset=POOL_BYTES + 4096, align_bytes=64)
+        nc.vector.tensor_tensor(factor_turned[:], size_turned[:], signed_os[:], ALU.mult)
         mean_turned = keep.tile([P, P], F32, name="mean_turned", tag="mean_turned", align_bytes=64)
         nc.vector.tensor_tensor(mean_turned[:], tp_sum[:], share_turned[:], ALU.mult)
         mean = turn_back(mean_turned, "mean", "a0")
-        share = turn_back(share_turned, "share", "back")
+        factor = turn_back(factor_turned, "factor", "back")
         turn_values(1, listed1, "val_a", nc.vector.tensor_copy)
         turn_values(2, gather_values(2), "val_b", nc.scalar.copy)
-        factor = keep.tile([P, G, 1, PACK], F32, name="factor")
-        nc.vector.tensor_tensor(factor[:, :, 0, :], share[:, 0, :, :], os_t[:].to_broadcast([P, G, PACK]), ALU.mult)
         quantise_values(0, 2)
-        pull = keep.tile([P, TEAM, G, PACK], F32, name="pull")
-        centred = keep.tile([P, TEAM, G, PACK], F32, name="centred", tag="centred", align_bytes=64)
-        for h in range(2):
+        team_halves = [slice(h * G // 2, (h + 1) * G // 2) for h in range(2)]
+        centred = []
+        for h, teams in enumerate(team_halves):
+            pull = keep.tile([P, TEAM, G // 2, PACK], F32, name=f"pull{h}")
             nc.vector.tensor_tensor(
-                pull[:, halves[h], :, :], mean[:].to_broadcast([P, HALF, G, PACK]), p_all[:, halves[h], :, :], ALU.mult
+                pull[:], mean[:, :, teams, :].to_broadcast([P, TEAM, G // 2, PACK]), p_all[:, :, teams, :], ALU.mult
             )
-        for h in range(2):
-            nc.vector.tensor_tensor(
-                centred[:, halves[h], :, :], tp_all[:, halves[h], :, :], pull[:, halves[h], :, :], ALU.subtract
+            centred.append(
+                keep.tile([P, TEAM, G // 2, PACK], F32, name=f"centred{h}", tag=f"centred{h}", align_bytes=64)
             )
+            nc.gpsimd.tensor_tensor(centred[h][:], tp_all[:, :, teams, :], pull[:], ALU.subtract)
         turn_values(3, gather_values(3), "val_a", nc.scalar.copy)
-        val_codes.append(
-            shared.tile([P, 2 * P], U32, name="val_codes1", offset=3 * POOL_BYTES + 4096, align_bytes=64)
-        )
-        quantise_values(2, 1)
         w_grouped = shared.tile(
             [P, 2, G // 2, TEAM, PACK], BF16, name="w_grouped", offset=3 * POOL_BYTES, align_bytes=64
         )
-        for h in range(2):
-            teams = slice(h * G // 2, (h + 1) * G // 2)
+        for h, teams in enumerate(team_halves):
             nc.vector.tensor_tensor(
                 w_grouped[:, h, :, :, :],
-                centred[:].rearrange("p j g t -> p g j t")[:, teams, :, :],
-                factor[:, teams, :, :].to_broadcast([P, G // 2, TEAM, PACK]),
+                factor[:].rearrange("p o g t -> p g o t")[:, teams, :, :].to_broadcast([P, G // 2, TEAM, PACK]),
+                centred[h][:].rearrange("p j g t -> p g j t"),
                 ALU.mult,
             )
         w_mx = [quantise(w_grouped[:, 0, :, :, :].rearrange("p g j t -> p (g j t)"), P, "w0")]
-        quantise_values(3, 1)
+        val_codes.append(keep.tile([P, 2 * P], U32, name="val_codes1", tag="centred1", align_bytes=64))
+        quantise_values(2, 2)
         w_mx.append(quantise(w_grouped[:, 1, :, :, :].rearrange("p g j t -> p (g j t)"), P, "w1"))
 
         for h in range(2):

from contextlib import ExitStack

import concourse.mybir as mybir
from concourse.masks import make_identity

D, E, T, I, Q, G = 512, 512, 2048, 512, 256, 32
FLOPS = 2 * (2 * D * I * Q + I * Q * E)

F32 = mybir.dt.float32
BF16 = mybir.dt.bfloat16
I32 = mybir.dt.int32
U32 = mybir.dt.uint32
U16 = mybir.dt.uint16
U8 = mybir.dt.uint8
FP8X4 = mybir.dt.float8_e4m3fn_x4
ALU = mybir.AluOpType
ACT = mybir.ActivationFunctionType

P = 128
PACK = 4
TEAM = Q // G
HALF = TEAM // 2
POOL_BYTES = T * 4


def tile_attend_ttteamshares_kernel(tc, query, dquery, keys_words, keys_scales, reserve, slot_factor, vals, offs, out):
    nc = tc.nc
    with ExitStack() as ctx:
        keep = ctx.enter_context(tc.tile_pool(name="keep", bufs=1))
        shared = ctx.enter_context(tc.tile_pool(name="shared", bufs=1))
        psum = ctx.enter_context(tc.psum_pool(name="psum", bufs=1))

        offsets = keep.tile([P, I // 16], U16, name="offsets")
        nc.sync.dma_start(offsets[:], offs)

        key_scale_pool = keep.tile([P, T], U8, name="key_scale_pool", align_bytes=64)
        nc.vector.memset(key_scale_pool[:].bitcast(I32), 0)
        for row in range(4):
            nc.sync.dma_start(
                key_scale_pool[row:P:32, :].bitcast(I32),
                keys_scales[0, row:16:4, :].bitcast(I32),
            )
        q_raw = keep.tile([P, PACK, Q], F32, name="q_raw")
        nc.sync.dma_start(q_raw[:], query.rearrange("(p t) q -> p t q", t=PACK))
        key_pool = keep.tile([P, T], I32, name="key_pool")
        nc.sync.dma_start(key_pool[:], keys_words[0].rearrange("p n t -> p (n t)").bitcast(I32))
        dq_raw = keep.tile([P, PACK, Q], F32, name="dq_raw")
        nc.sync.dma_start(dq_raw[:], dquery.rearrange("(p t) q -> p t q", t=PACK))
        val_pools = []
        for k in range(E // P):
            val_pool = shared.tile([P, T], F32, name=f"val_pool{k}", offset=k * POOL_BYTES, align_bytes=64)
            nc.sync.dma_start(val_pool[:], vals[k * P : (k + 1) * P, :])
            val_pools.append(val_pool)

        reserve_t = keep.tile([P, 1, PACK], F32, name="reserve_t")
        nc.gpsimd.dma_start(reserve_t[:], reserve.rearrange("(p t) o -> p o t", t=PACK))
        os_t = keep.tile([P, 1, PACK], F32, name="os_t", tag="os_t", align_bytes=64)
        nc.gpsimd.dma_start(os_t[:], slot_factor.rearrange("(p t) o -> p o t", t=PACK))
        identity = keep.tile([P, P], F32, name="identity")
        make_identity(nc, identity[:])
        reserve_wide = keep.tile([P, G, PACK], F32, name="reserve_wide", tag="reserve_wide", align_bytes=64)
        nc.gpsimd.tensor_copy(reserve_wide[:], reserve_t[:].to_broadcast([P, G, PACK]))

        os_wide = keep.tile([P, G, PACK], F32, name="os_wide")
        nc.gpsimd.tensor_copy(os_wide[:], os_t[:].to_broadcast([P, G, PACK]))
        os_bank = psum.tile([P, P], F32, name="os_bank", tag="back")
        nc.tensor.transpose(os_bank[:], os_wide[:].rearrange("p g t -> p (g t)"), identity[:])
        os_turned = keep.tile([P, P], F32, name="os_turned")
        nc.scalar.copy(os_turned[:], os_bank[:])
        key_scales_listed = keep.tile([P, I], U8, name="key_scales_listed", align_bytes=64)
        nc.vector.tensor_copy(key_scales_listed[:], key_scale_pool[:].indirect(offsets[:]))
        key_scales = keep.tile([P, PACK, P], U8, name="key_scales", align_bytes=64)
        nc.vector.tensor_copy(
            key_scales[:].rearrange("p t (a b) -> p a t b", b=16),
            key_scales_listed[:].rearrange("p (a b t) -> p a t b", b=16, t=PACK),
        )

        def interleave(copy, raw, name):
            grouped = keep.tile([P, Q * PACK], BF16, name=name, align_bytes=64)
            copy(
                grouped[:].rearrange("p (h g l t) -> p h g t l", h=2, l=HALF, t=PACK),
                raw[:].rearrange("p t (g h l) -> p h g t l", h=2, l=HALF),
            )
            return grouped

        def quantise(grouped, width, name, offset=None):
            if offset is None:
                codes = keep.tile([P, width], U32, name=name + "_codes", align_bytes=64)
            else:
                codes = shared.tile([P, width], U32, name=name + "_codes", offset=offset, align_bytes=64)
            scales = keep.tile([P, width], U8, name=name + "_scales", align_bytes=64)
            nc.vector.quantize_mx(out=codes[:].bitcast(FP8X4), scales=scales[:], in_=grouped)
            return codes, scales

        q_grouped = interleave(nc.scalar.copy, q_raw, "q_grouped")
        q_codes, q_scales = quantise(q_grouped[:], Q, "q")

        key_codes = keep.tile([P, PACK, P], U32, name="key_codes", align_bytes=64)
        nc.vector.tensor_copy(
            key_codes[:].rearrange("p t s -> p s t"), key_pool[:].bitcast(U32).indirect(offsets[:])
        )

        def scores(codes, scales, tag):
            banks = []
            for h in range(2):
                bank = psum.tile([P, PACK, P], F32, name=f"{tag}{h}", tag=f"{tag}{h}")
                for t in range(PACK):
                    nc.tensor.matmul_mx(
                        out=bank[:, t, :],
                        lhsT=key_codes[:, t, :].bitcast(FP8X4),
                        lhsT_scale=key_scales[:, t, :],
                        rhs=codes[:, h * P : (h + 1) * P].bitcast(FP8X4),
                        rhs_scale=scales[:, h * P : (h + 1) * P],
                        start=True,
                        stop=True,
                    )
                banks.append(bank[:].rearrange("p t (g l) -> p l g t", l=HALF))
            return banks

        a_banks = scores(q_codes, q_scales, "a")
        dq_grouped = interleave(nc.vector.tensor_copy, dq_raw, "dq_grouped")
        dq_codes, dq_scales = quantise(dq_grouped[:], Q, "dq")
        ta_banks = scores(dq_codes, dq_scales, "ta")

        p_all = keep.tile([P, TEAM, G, PACK], F32, name="p_all", tag="p_all", align_bytes=64)
        halves = [slice(h * HALF, (h + 1) * HALF) for h in range(2)]
        for h in range(2):
            nc.scalar.activation(p_all[:, halves[h], :, :], a_banks[h], ACT.Exp)

        def team_sum(members, name, tag):
            turned = psum.tile([P, P], F32, name=name + "_turned", tag=tag)
            for n, member in enumerate(members):
                nc.tensor.matmul(
                    turned[:], member, identity[:], is_transpose=True, start=(n == 0), stop=(n == len(members) - 1)
                )
            return turned

        def turn_back(turned, name, tag):
            back = psum.tile([P, 1, G, PACK], F32, name=name, tag=tag)
            nc.tensor.transpose(back[:].rearrange("p o g t -> p (o g t)"), turned[:], identity[:])
            return back

        def members_of(tile):
            return [tile[:, j, :, :].rearrange("p g t -> p (g t)") for j in range(TEAM)]

        val_grouped = keep.tile([P, E * PACK], BF16, name="val_grouped", align_bytes=64)
        val_scales = keep.tile([P, E], U8, name="val_scales", align_bytes=64)
        val_codes = [keep.tile([P, 2 * P], U32, name="val_codes0", align_bytes=64)]

        def quantise_values(first, count):
            nc.vector.quantize_mx(
                out=val_codes[first // 2][:, first % 2 * P : (first % 2 + count) * P].bitcast(FP8X4),
                scales=val_scales[:, first * P : (first + count) * P],
                in_=val_grouped[:, first * P * PACK : (first + count) * P * PACK],
            )

        def gather_values(k):
            listed = keep.tile([P, I], BF16, name=f"val_listed{k}", tag=["val_listed0", "reserve_wide", "val_listed2", "p_all"][k], align_bytes=64)
            if k == 2:
                rounded = keep.tile([P, T], BF16, name="val_rounded", tag="val_listed0", align_bytes=64)
                nc.scalar.activation(rounded[:], val_pools[k][:], ACT.Copy)
                nc.scalar.activation(listed[:], rounded[:].indirect(offsets[:]), ACT.Copy)
            else:
                nc.vector.tensor_copy(listed[:], val_pools[k][:].indirect(offsets[:]))
            return listed

        def turn_values(k, listed, bank_tag, copy_out):
            words = listed[:].bitcast(F32)
            turned = psum.tile([P, 2, P], F32, name=f"val_turned{k}", tag=bank_tag)
            for u in range(2):
                nc.tensor.transpose(turned[:, u, :], words[:, u::2], identity[:])
            copy_out(
                val_grouped[:, k * P * PACK : (k + 1) * P * PACK].bitcast(F32).rearrange("p (e u) -> p e u", u=2),
                turned[:].rearrange("p u e -> p e u"),
            )

        den = team_sum(members_of(p_all) + [reserve_wide[:].rearrange("p g t -> p (g t)")], "den", "den")
        root_turned = keep.tile([P, P], F32, name="root_turned")
        nc.scalar.activation(root_turned[:], den[:], ACT.Abs_reciprocal_sqrt)
        sign_turned = keep.tile([P, P], F32, name="sign_turned")
        nc.scalar.activation(sign_turned[:], den[:], ACT.Sign)
        size_turned = keep.tile([P, P], F32, name="size_turned", tag="size_turned", align_bytes=64)
        nc.scalar.activation(size_turned[:], root_turned[:], ACT.Square)
        signed_os = keep.tile([P, P], F32, name="signed_os")
        nc.gpsimd.tensor_tensor(signed_os[:], sign_turned[:], os_turned[:], ALU.mult)
        turn_values(0, gather_values(0), "den", nc.scalar.copy)
        tp_all = shared.tile([P, TEAM, G, PACK], F32, name="tp_all", offset=0, align_bytes=64)
        for h in range(2):
            nc.vector.tensor_tensor(tp_all[:, halves[h], :, :], ta_banks[h], p_all[:, halves[h], :, :], ALU.mult)
        tp_sum = team_sum(members_of(tp_all), "tp", "a1")
        listed1 = gather_values(1)
        share_turned = shared.tile([P, P], F32, name="share_turned", offset=POOL_BYTES + 2048, align_bytes=64)
        nc.vector.tensor_tensor(share_turned[:], size_turned[:], sign_turned[:], ALU.mult)
        factor_turned = shared.tile([P, P], F32, name="factor_turned", offset=POOL_BYTES + 4096, align_bytes=64)
        nc.vector.tensor_tensor(factor_turned[:], size_turned[:], signed_os[:], ALU.mult)
        mean_turned = keep.tile([P, P], F32, name="mean_turned", tag="mean_turned", align_bytes=64)
        nc.vector.tensor_tensor(mean_turned[:], tp_sum[:], share_turned[:], ALU.mult)
        mean = turn_back(mean_turned, "mean", "a0")
        factor = turn_back(factor_turned, "factor", "back")
        turn_values(1, listed1, "val_a", nc.vector.tensor_copy)
        turn_values(2, gather_values(2), "val_b", nc.scalar.copy)
        quantise_values(0, 2)
        team_halves = [slice(h * G // 2, (h + 1) * G // 2) for h in range(2)]
        centred = []
        for h, teams in enumerate(team_halves):
            pull = keep.tile([P, TEAM, G // 2, PACK], F32, name=f"pull{h}")
            nc.vector.tensor_tensor(
                pull[:], mean[:, :, teams, :].to_broadcast([P, TEAM, G // 2, PACK]), p_all[:, :, teams, :], ALU.mult
            )
            centred.append(
                keep.tile([P, TEAM, G // 2, PACK], F32, name=f"centred{h}", tag=f"centred{h}", align_bytes=64)
            )
            nc.gpsimd.tensor_tensor(centred[h][:], tp_all[:, :, teams, :], pull[:], ALU.subtract)
        turn_values(3, gather_values(3), "val_a", nc.scalar.copy)
        w_grouped = shared.tile(
            [P, 2, G // 2, TEAM, PACK], BF16, name="w_grouped", offset=3 * POOL_BYTES, align_bytes=64
        )
        for h, teams in enumerate(team_halves):
            nc.vector.tensor_tensor(
                w_grouped[:, h, :, :, :],
                factor[:].rearrange("p o g t -> p g o t")[:, teams, :, :].to_broadcast([P, G // 2, TEAM, PACK]),
                centred[h][:].rearrange("p j g t -> p g j t"),
                ALU.mult,
            )
        w_mx = [quantise(w_grouped[:, 0, :, :, :].rearrange("p g j t -> p (g j t)"), P, "w0")]
        val_codes.append(keep.tile([P, 2 * P], U32, name="val_codes1", tag="centred1", align_bytes=64))
        quantise_values(2, 2)
        w_mx.append(quantise(w_grouped[:, 1, :, :, :].rearrange("p g j t -> p (g j t)"), P, "w1"))

        for h in range(2):
            for n in range(2):
                bank = psum.tile([P, 2 * P], F32, name=f"out_bank{h}{n}", tag=["ta0", "ta1", "a0", "a1"][2 * h + n])
                nc.tensor.matmul_mx(
                    out=bank[:],
                    lhsT=w_mx[h][0][:].bitcast(FP8X4),
                    lhsT_scale=w_mx[h][1][:],
                    rhs=val_codes[n][:].bitcast(FP8X4),
                    rhs_scale=val_scales[:, n * 2 * P : (n + 1) * 2 * P],
                    start=True,
                    stop=True,
                )
                copy = nc.vector.tensor_copy if n == 1 else nc.scalar.copy
                result = keep.tile([P, 2 * P], F32, name=f"result{h}{n}")
                copy(result[:], bank[:])
                nc.sync.dma_start(out[h * P : (h + 1) * P, n * 2 * P : (n + 1) * 2 * P], result[:])
